import numpy as np, ml_dtypes
CORES = [78,86,94,102,110,118]
N = 6
import mx_ref
NC, G = 256, 2
C = np.float32(0.041)
BF = ml_dtypes.bfloat16
def cut(t, i, w=512):
    return t[:, w * i:w * i + w]
def tile(rs):
    return np.stack(rs, axis=2).reshape(128, -1).astype(BF)
def fold(P):
    return [f(p, axis=0) * C for p in P for f in (np.max, np.min)]
def setup_inputs(rng):
    def f(*shape):
        return mx_ref.flush((rng.standard_normal(shape, dtype=np.float32) * np.exp2(rng.integers(-2, 3, shape[:-1] + (1,)))).astype(BF))
    return {"x": f(N, 128, 4 * NC), "w1": f(N, 128, G * 512), "w2": f(N, 128, 2 * 512)}
def setup_inputs_blocks(rng):
    d = setup_inputs(rng)
    for k in ("x", "w1", "w2"): d[k] = mx_ref.spread(d[k], rng, 4)
    return d
def setup_inputs_wide(rng):
    d = setup_inputs(rng)
    for k in ("x", "w1", "w2"): d[k] = mx_ref.flush((d[k].astype(np.float32) * np.exp2(rng.integers(-8, 9, (N, 1, 1))).astype(np.float32)).astype(BF))
    return d
def reference(x, w1, w2, own=None):
    X = [mx_ref.quantize(x[j]) for j in range(N)]
    h = np.stack([tile(fold([[mx_ref.matmul(mx_ref.quantize(cut(w1[r], i)), X[j]) for j in range(N)] for i in range(G)])) for r in range(N)])
    use = h if own is None else own["h"]
    H = [mx_ref.quantize(use[j]) for j in range(N)]
    y = np.zeros((N, 128, NC), np.float32)
    for r in range(N):
        y[r] = mx_ref.matmul(mx_ref.quantize(cut(w2[r], 0)), H[r]) + mx_ref.matmul(mx_ref.quantize(cut(w2[r], 1)), H[(r + 1) % N])
    return {"h": h, "y": y}

@@ -1,0 +1,176 @@
+from concourse.mybir import dt, AluOpType, ActivationFunctionType
+
+N = 6
+NCORES = 128
+NC = 256
+SCALE = 0.041
+
+DIRECT = (1, 2, 3, 4, 5)
+RELAY = ()
+ORDER = (1, 2, 3, 4, 5)
+RING = 3
+YBANK = 2 * RING
+
+SCRATCH = {
+    "xb": ("sbuf", [128, 4 * NC], "bfloat16"),
+    "w1b": ("sbuf", [128, 1024], "bfloat16"),
+    "w2b": ("sbuf", [128, 1024], "bfloat16"),
+    "xq": ("sbuf", [128, N * NC], "float8_e4m3fn_x4"),
+    "xs": ("sbuf", [128, N * NC], "uint8"),
+    "w1q": ("sbuf", [128, 256], "float8_e4m3fn_x4"),
+    "w1s": ("sbuf", [128, 256], "uint8"),
+    "w2q": ("sbuf", [128, 256], "float8_e4m3fn_x4"),
+    "w2s": ("sbuf", [128, 256], "uint8"),
+    "acc": ("sbuf", [128, 2 * NC], "float32"),
+    "mx": ("sbuf", [128, 2 * NC], "float32"),
+    "mn": ("sbuf", [128, 2 * NC], "float32"),
+    "hb": ("sbuf", [128, 4 * NC], "bfloat16"),
+    "hq": ("sbuf", [128, 2 * NC], "float8_e4m3fn_x4"),
+    "hs": ("sbuf", [128, 2 * NC], "uint8"),
+    "yb": ("sbuf", [128, NC], "float32"),
+    "ps": ("psum", [128, 512 * (YBANK + 1)], "float32"),
+}
+SEMAPHORES = (["ldx", "ldw1", "ldw2", "qx", "qw1", "qw2", "qh", "loc", "ah", "sc", "ymm", "yc", "sty", "sth"]
+              + ["ax%d" % j for j in range(N)]
+              + ["%s%d" % (s, i) for s in ("cp", "mx", "mn") for i in range(2)]
+              + ["mm%d_%d" % (i, n) for i in range(2) for n in range(N)])
+
+
+def _count(mask):
+    return bin(mask).count("1")
+
+
+def _helpers(T, topo, r):
+    core = T.cores[r]
+    free = [c for c in range(NCORES) if topo.chip(c) == topo.chip(core) and T.rank_of(c) is None]
+    free.sort(key=lambda c: (topo.die(c) == topo.die(core), c))
+    out = []
+    for offs in RELAY:
+        c = [c for c in free if c not in out and all(topo.may_write(c, T.cores[(r + k) % N]) for k in offs)][0]
+        out.append(c)
+    return out
+
+
+def _send(g, T, topo, src, dst, q, s, a_src, a_dst, sem):
+    rid, pid, _ = topo.addr(dst)
+    m = topo.mask(src, dst)
+    g.remote_dma(out_ap=T[q][:, a_dst:a_dst + NC].bitcast(dt.uint8), in_ap=T[q][:, a_src:a_src + NC].bitcast(dt.uint8),
+                 remote_sem=sem, local_sem=T.sem.loc, pid=pid, routing_id=rid, dma_engine_mask=m)
+    g.remote_dma(out_ap=T[s][:, a_dst:a_dst + NC], in_ap=T[s][:, a_src:a_src + NC],
+                 remote_sem=sem, local_sem=T.sem.loc, pid=pid, routing_id=rid, dma_engine_mask=m)
+    return 2 * _count(m)
+
+
+def _relay_program(g, core, T, topo):
+    for r in range(N):
+        hs = _helpers(T, topo, r)
+        if core not in hs:
+            continue
+        a = r * NC
+        sem = T.sem["ax%d" % r]
+        g.wait_ge(sem, 2 * _count(topo.mask(T.cores[r], core)))
+        sent = 0
+        for k in RELAY[hs.index(core)]:
+            sent += _send(g, T, topo, core, T.cores[(r + k) % N], "xq", "xs", a, a, sem)
+        g.wait_ge(T.sem.loc, sent)
+
+
+def rank_program(g, core, T, topo):
+    rank = T.rank_of(core)
+    if rank is None:
+        _relay_program(g, core, T, topo)
+        return
+    S = T.sem
+    v, te, sc, sy = g.vector, g.tensor, g.scalar, g.sync
+    own = rank * NC
+    helpers = _helpers(T, topo, rank)
+
+    def bank(i, n):
+        b = 512 * (2 * (n % RING) + i)
+        return T.ps[:, b:b + NC]
+
+    def half(name, i):
+        return T[name][:, i * NC:(i + 1) * NC]
+
+    sy.dma_start(T.xb[:], T.x[:]).then_inc(S.ldx, 16)
+    sy.dma_start(T.w1b[:], T.w1[:]).then_inc(S.ldw1, 16)
+    sy.dma_start(T.w2b[:], T.w2[:]).then_inc(S.ldw2, 16)
+
+    v.wait_ge(S.ldx, 16)
+    v.quantize_mx(T.xq[:, own:own + NC], T.xs[:, own:own + NC], T.xb[:]).then_inc(S.qx, 1)
+    v.wait_ge(S.ldw1, 16)
+    v.quantize_mx(T.w1q[:], T.w1s[:], T.w1b[:]).then_inc(S.qw1, 1)
+    v.wait_ge(S.ldw2, 16)
+    v.quantize_mx(T.w2q[:], T.w2s[:], T.w2b[:]).then_inc(S.qw2, 1)
+
+    g.wait_ge(S.qx, 1)
+    sent = 0
+    for c in helpers:
+        sent += _send(g, T, topo, core, c, "xq", "xs", own, own, S["ax%d" % rank])
+    for k in DIRECT:
+        sent += _send(g, T, topo, core, T.cores[(rank + k) % N], "xq", "xs", own, own, S["ax%d" % rank])
+
+    te.wait_ge(S.qx, 1)
+    te.wait_ge(S.qw1, 1)
+    srcs = [rank] + [(rank - k) % N for k in ORDER]
+    for n, j in enumerate(srcs):
+        if n:
+            k = (rank - j) % N
+            sender = T.cores[j]
+            for c, offs in zip(_helpers(T, topo, j), RELAY):
+                if k in offs:
+                    sender = c
+            te.wait_ge(S["ax%d" % j], 2 * _count(topo.mask(sender, core)))
+        for i in range(2):
+            if n == RING:
+                te.wait_ge(S["cp%d" % i], 1)
+            elif n > RING:
+                te.wait_ge(S["mx%d" % i], n - RING)
+                te.wait_ge(S["mn%d" % i], n - RING)
+            te.matmul_mx(bank(i, n), T.w1q[:, 128 * i:128 * i + 128], T.w1s[:, 128 * i:128 * i + 128],
+                         T.xq[:, j * NC:(j + 1) * NC], T.xs[:, j * NC:(j + 1) * NC], True, True).then_inc(S["mm%d_%d" % (i, n)], 1)
+
+    for i in range(2):
+        sc.wait_ge(S["mm%d_0" % i], 1)
+        sc.activation(half("acc", i), bank(i, 0), ActivationFunctionType.Copy).then_inc(S["cp%d" % i], 1)
+
+    for n in range(1, N):
+        for i in range(2):
+            v.wait_ge(S["mm%d_%d" % (i, n)], 1)
+            for name, op in (("mx", AluOpType.max), ("mn", AluOpType.min)):
+                if n == 1:
+                    v.wait_ge(S["cp%d" % i], 1)
+                    prev = half("acc", i)
+                else:
+                    v.wait_ge(S["%s%d" % (name, i)], n - 1)
+                    prev = half(name, i)
+                v.tensor_tensor(half(name, i), bank(i, n), prev, op).then_inc(S["%s%d" % (name, i)], 1)
+
+    for b, (name, i) in enumerate((("mx", 0), ("mn", 0), ("mx", 1), ("mn", 1))):
+        sc.wait_ge(S["%s%d" % (name, i)], N - 1)
+        sc.activation(T.hb[:, b:4 * NC:4], half(name, i), ActivationFunctionType.Copy, scale=SCALE).then_inc(S.sc, 1)
+
+    v.wait_ge(S.sc, 4)
+    v.quantize_mx(T.hq[:, 0:NC], T.hs[:, 0:NC], T.hb[:]).then_inc(S.qh, 1)
+
+    g.wait_ge(S.qh, 1)
+    sent += _send(g, T, topo, core, T.cores[(rank - 1) % N], "hq", "hs", 0, NC, S.ah)
+    g.wait_ge(S.loc, sent)
+
+    sc.wait_ge(S.sc, 4)
+    sc.wait_ge(S.loc, sent)
+    sc.dma_start(T.h[:], T.hb[:]).then_inc(S.sth, 16)
+
+    te.wait_ge(S.qw2, 1)
+    te.wait_ge(S.qh, 1)
+    yp = T.ps[:, 512 * YBANK:512 * YBANK + NC]
+    te.matmul_mx(yp, T.w2q[:, 0:128], T.w2s[:, 0:128], T.hq[:, 0:NC], T.hs[:, 0:NC], True, False)
+    te.wait_ge(S.ah, 2 * _count(topo.mask(T.cores[(rank + 1) % N], core)))
+    te.matmul_mx(yp, T.w2q[:, 128:256], T.w2s[:, 128:256], T.hq[:, NC:2 * NC], T.hs[:, NC:2 * NC], False, True).then_inc(S.ymm, 1)
+
+    v.wait_ge(S.ymm, 1)
+    v.tensor_copy(T.yb[:], yp).then_inc(S.yc, 1)
+    sy.wait_ge(S.yc, 1)
+    sy.dma_start(T.y[:], T.yb[:]).then_inc(S.sty, 16)
+    sy.wait_ge(S.sty, 16)
+    sc.wait_ge(S.sth, 16)

@@ -3,13 +3,17 @@ from concourse.mybir import dt, AluOpType, ActivationFunctionType
 N = 6
 NCORES = 128
 NC = 256
+HC = NC // 2
 SCALE = 0.041
 
-DIRECT = (1, 2, 3, 4, 5)
-RELAY = ()
+DIRECT = (1, 2, 3, 5)
+RELAY = ((4,),)
+FIRST = 1
 ORDER = (1, 2, 3, 4, 5)
 RING = 3
 YBANK = 2 * RING
+FOLDS = (("mx", AluOpType.max), ("mn", AluOpType.min))
+PARTS = (("mx", 0), ("mn", 0), ("mx", 1), ("mn", 1))
 
 SCRATCH = {
     "xb": ("sbuf", [128, 4 * NC], "bfloat16"),
@@ -28,9 +32,10 @@ SCRATCH = {
     "hq": ("sbuf", [128, 2 * NC], "float8_e4m3fn_x4"),
     "hs": ("sbuf", [128, 2 * NC], "uint8"),
     "yb": ("sbuf", [128, NC], "float32"),
-    "ps": ("psum", [128, 512 * (YBANK + 1)], "float32"),
+    "ps": ("psum", [128, 512 * (YBANK + 2)], "float32"),
 }
-SEMAPHORES = (["ldx", "ldw1", "ldw2", "qx", "qw1", "qw2", "qh", "loc", "ah", "sc", "ymm", "yc", "sty", "sth"]
+SEMAPHORES = (["ldx", "ldw1", "ldw2", "qx", "qw1", "qw2", "qh", "loc", "ah", "sc0", "sc1", "ym0", "ym1", "yc", "sty", "sth",
+               "rs", "rc"]
               + ["ax%d" % j for j in range(N)]
               + ["%s%d" % (s, i) for s in ("cp", "mx", "mn") for i in range(2)]
               + ["mm%d_%d" % (i, n) for i in range(2) for n in range(N)])
@@ -51,14 +56,23 @@ def _helpers(T, topo, r):
     return out
 
 
-def _send(g, T, topo, src, dst, q, s, a_src, a_dst, sem):
+def _put(g, T, topo, src, dst, buf, a_src, a_dst, sem, mask=None):
     rid, pid, _ = topo.addr(dst)
-    m = topo.mask(src, dst)
-    g.remote_dma(out_ap=T[q][:, a_dst:a_dst + NC].bitcast(dt.uint8), in_ap=T[q][:, a_src:a_src + NC].bitcast(dt.uint8),
-                 remote_sem=sem, local_sem=T.sem.loc, pid=pid, routing_id=rid, dma_engine_mask=m)
-    g.remote_dma(out_ap=T[s][:, a_dst:a_dst + NC], in_ap=T[s][:, a_src:a_src + NC],
-                 remote_sem=sem, local_sem=T.sem.loc, pid=pid, routing_id=rid, dma_engine_mask=m)
-    return 2 * _count(m)
+    m = topo.mask(src, dst) if mask is None else mask
+    o, i = T[buf][:, a_dst:a_dst + NC], T[buf][:, a_src:a_src + NC]
+    if buf in ("xq", "hq"):
+        o, i = o.bitcast(dt.uint8), i.bitcast(dt.uint8)
+    g.remote_dma(out_ap=o, in_ap=i, remote_sem=sem, local_sem=T.sem.loc, pid=pid, routing_id=rid, dma_engine_mask=m)
+    return _count(m)
+
+
+def _chip_mask(T, topo, core, helper):
+    on = topo.mask(core, helper)
+    off = 0
+    for c in T.cores:
+        if topo.chip(c) != topo.chip(core):
+            off |= topo.mask(core, c)
+    return (on & ~off) or on
 
 
 def _relay_program(g, core, T, topo):
@@ -67,11 +81,12 @@ def _relay_program(g, core, T, topo):
         if core not in hs:
             continue
         a = r * NC
-        sem = T.sem["ax%d" % r]
-        g.wait_ge(sem, 2 * _count(topo.mask(T.cores[r], core)))
+        n = _count(_chip_mask(T, topo, T.cores[r], core))
         sent = 0
-        for k in RELAY[hs.index(core)]:
-            sent += _send(g, T, topo, core, T.cores[(r + k) % N], "xq", "xs", a, a, sem)
+        for buf, sem in (("xs", T.sem.rs), ("xq", T.sem.rc)):
+            g.wait_ge(sem, n)
+            for k in RELAY[hs.index(core)]:
+                sent += _put(g, T, topo, core, T.cores[(r + k) % N], buf, a, a, T.sem["ax%d" % r])
         g.wait_ge(T.sem.loc, sent)
 
 
@@ -85,12 +100,12 @@ def rank_program(g, core, T, topo):
     own = rank * NC
     helpers = _helpers(T, topo, rank)
 
-    def bank(i, n):
-        b = 512 * (2 * (n % RING) + i)
-        return T.ps[:, b:b + NC]
+    def bank(i, n, a=0, b=NC):
+        c = 512 * (2 * (n % RING) + i)
+        return T.ps[:, c + a:c + b]
 
-    def half(name, i):
-        return T[name][:, i * NC:(i + 1) * NC]
+    def part(name, i, a=0, b=NC):
+        return T[name][:, i * NC + a:i * NC + b]
 
     sy.dma_start(T.xb[:], T.x[:]).then_inc(S.ldx, 16)
     sy.dma_start(T.w1b[:], T.w1[:]).then_inc(S.ldw1, 16)
@@ -105,10 +120,13 @@ def rank_program(g, core, T, topo):
 
     g.wait_ge(S.qx, 1)
     sent = 0
-    for c in helpers:
-        sent += _send(g, T, topo, core, c, "xq", "xs", own, own, S["ax%d" % rank])
-    for k in DIRECT:
-        sent += _send(g, T, topo, core, T.cores[(rank + k) % N], "xq", "xs", own, own, S["ax%d" % rank])
+    for n, k in enumerate(DIRECT):
+        if n == FIRST:
+            for buf, sem in (("xs", S.rs), ("xq", S.rc)):
+                for c in helpers:
+                    sent += _put(g, T, topo, core, c, buf, own, own, sem, _chip_mask(T, topo, core, c))
+        for buf in ("xq", "xs"):
+            sent += _put(g, T, topo, core, T.cores[(rank + k) % N], buf, own, own, S["ax%d" % rank])
 
     te.wait_ge(S.qx, 1)
     te.wait_ge(S.qw1, 1)
@@ -132,45 +150,67 @@ def rank_program(g, core, T, topo):
 
     for i in range(2):
         sc.wait_ge(S["mm%d_0" % i], 1)
-        sc.activation(half("acc", i), bank(i, 0), ActivationFunctionType.Copy).then_inc(S["cp%d" % i], 1)
+        sc.activation(part("acc", i), bank(i, 0), ActivationFunctionType.Copy).then_inc(S["cp%d" % i], 1)
 
-    for n in range(1, N):
+    for n in range(1, N - 1):
         for i in range(2):
             v.wait_ge(S["mm%d_%d" % (i, n)], 1)
-            for name, op in (("mx", AluOpType.max), ("mn", AluOpType.min)):
+            for name, op in FOLDS:
                 if n == 1:
                     v.wait_ge(S["cp%d" % i], 1)
-                    prev = half("acc", i)
+                    prev = part("acc", i)
                 else:
                     v.wait_ge(S["%s%d" % (name, i)], n - 1)
-                    prev = half(name, i)
-                v.tensor_tensor(half(name, i), bank(i, n), prev, op).then_inc(S["%s%d" % (name, i)], 1)
+                    prev = part(name, i)
+                v.tensor_tensor(part(name, i), bank(i, n), prev, op).then_inc(S["%s%d" % (name, i)], 1)
+    n = N - 1
+    for f in range(2):
+        for i in range(2):
+            v.wait_ge(S["mm%d_%d" % (i, n)], 1)
+            for name, op in FOLDS:
+                v.wait_ge(S["%s%d" % (name, i)], n - 1 + f)
+                m = part(name, i, f * HC, (f + 1) * HC)
+                v.tensor_tensor(m, bank(i, n, f * HC, (f + 1) * HC), m, op).then_inc(S["%s%d" % (name, i)], 1)
 
-    for b, (name, i) in enumerate((("mx", 0), ("mn", 0), ("mx", 1), ("mn", 1))):
-        sc.wait_ge(S["%s%d" % (name, i)], N - 1)
-        sc.activation(T.hb[:, b:4 * NC:4], half(name, i), ActivationFunctionType.Copy, scale=SCALE).then_inc(S.sc, 1)
+    for f in range(2):
+        for b, (name, i) in enumerate(PARTS):
+            sc.wait_ge(S["%s%d" % (name, i)], N - 1 + f)
+            sc.activation(T.hb[:, 4 * HC * f + b:4 * HC * (f + 1):4], part(name, i, f * HC, (f + 1) * HC),
+                          ActivationFunctionType.Copy, scale=SCALE).then_inc(S["sc%d" % f], 1)
 
-    v.wait_ge(S.sc, 4)
-    v.quantize_mx(T.hq[:, 0:NC], T.hs[:, 0:NC], T.hb[:]).then_inc(S.qh, 1)
+    for f in range(2):
+        v.wait_ge(S["sc%d" % f], 4)
+        v.quantize_mx(T.hq[:, f * HC:(f + 1) * HC], T.hs[:, f * HC:(f + 1) * HC],
+                      T.hb[:, 4 * HC * f:4 * HC * (f + 1)]).then_inc(S.qh, 1)
 
-    g.wait_ge(S.qh, 1)
-    sent += _send(g, T, topo, core, T.cores[(rank - 1) % N], "hq", "hs", 0, NC, S.ah)
+    g.wait_ge(S.qh, 2)
+    for buf in ("hq", "hs"):
+        sent += _put(g, T, topo, core, T.cores[(rank - 1) % N], buf, 0, NC, S.ah)
     g.wait_ge(S.loc, sent)
 
-    sc.wait_ge(S.sc, 4)
+    sc.wait_ge(S.sc0, 4)
+    sc.wait_ge(S.sc1, 4)
     sc.wait_ge(S.loc, sent)
     sc.dma_start(T.h[:], T.hb[:]).then_inc(S.sth, 16)
 
     te.wait_ge(S.qw2, 1)
-    te.wait_ge(S.qh, 1)
-    yp = T.ps[:, 512 * YBANK:512 * YBANK + NC]
-    te.matmul_mx(yp, T.w2q[:, 0:128], T.w2s[:, 0:128], T.hq[:, 0:NC], T.hs[:, 0:NC], True, False)
-    te.wait_ge(S.ah, 2 * _count(topo.mask(T.cores[(rank + 1) % N], core)))
-    te.matmul_mx(yp, T.w2q[:, 128:256], T.w2s[:, 128:256], T.hq[:, NC:2 * NC], T.hs[:, NC:2 * NC], False, True).then_inc(S.ymm, 1)
+    te.wait_ge(S.qh, 2)
+    yp = [T.ps[:, 512 * (YBANK + f):512 * (YBANK + f) + HC] for f in range(2)]
+    for t in range(2):
+        if t:
+            te.wait_ge(S.ah, 2 * _count(topo.mask(T.cores[(rank + 1) % N], core)))
+        for f in range(2):
+            a = t * NC + f * HC
+            mm = te.matmul_mx(yp[f], T.w2q[:, 128 * t:128 * t + 128], T.w2s[:, 128 * t:128 * t + 128],
+                              T.hq[:, a:a + HC], T.hs[:, a:a + HC], t == 0, t == 1)
+            if t:
+                mm.then_inc(S["ym%d" % f], 1)
 
-    v.wait_ge(S.ymm, 1)
-    v.tensor_copy(T.yb[:], yp).then_inc(S.yc, 1)
-    sy.wait_ge(S.yc, 1)
+    v.wait_ge(S.ym0, 1)
+    v.tensor_copy(T.yb[:, 0:HC], yp[0]).then_inc(S.yc, 1)
+    sc.wait_ge(S.ym1, 1)
+    sc.activation(T.yb[:, HC:NC], yp[1], ActivationFunctionType.Copy).then_inc(S.yc, 1)
+    sy.wait_ge(S.yc, 2)
     sy.dma_start(T.y[:], T.yb[:]).then_inc(S.sty, 16)
     sy.wait_ge(S.sty, 16)
     sc.wait_ge(S.sth, 16)

@@ -1,3 +1,4 @@
+from concourse.bass import DstId, RemoteDMATransfer
 from concourse.mybir import dt, AluOpType, ActivationFunctionType
 
 N = 6
@@ -6,14 +7,14 @@ NC = 256
 HC = NC // 2
 SCALE = 0.041
 
-DIRECT = (1, 2, 3, 5)
-RELAY = ((4,),)
-FIRST = 1
-ORDER = (1, 2, 3, 4, 5)
+DIRECT = (1, 2, 5)
+RELAY = (3, 4)
+WORK = ((1, None), (2, None), (5, 0), (3, 0), (4, 0), (3, 1), (4, 1), (5, 1))
 RING = 3
 YBANK = 2 * RING
 FOLDS = (("mx", AluOpType.max), ("mn", AluOpType.min))
 PARTS = (("mx", 0), ("mn", 0), ("mx", 1), ("mn", 1))
+PIECES = ("xs", "xq")
 
 SCRATCH = {
     "xb": ("sbuf", [128, 4 * NC], "bfloat16"),
@@ -34,11 +35,12 @@ SCRATCH = {
     "yb": ("sbuf", [128, NC], "float32"),
     "ps": ("psum", [128, 512 * (YBANK + 2)], "float32"),
 }
-SEMAPHORES = (["ldx", "ldw1", "ldw2", "qx", "qw1", "qw2", "qh", "loc", "ah", "sc0", "sc1", "ym0", "ym1", "yc", "sty", "sth",
-               "rs", "rc"]
-              + ["ax%d" % j for j in range(N)]
+SEMAPHORES = (["ldx0", "ldx1", "ldw1", "ldw2", "qx0", "qx1", "qw1", "qw2", "qh0", "qh1", "loc", "ah0", "ah1", "sc0", "sc1",
+               "ym0", "ym1", "yc0", "yc1", "sty0", "sty1", "sth"]
+              + ["f%s" % p for p in PIECES]
+              + ["%sx%d" % (s, j) for s in "ab" for j in range(N)]
               + ["%s%d" % (s, i) for s in ("cp", "mx", "mn") for i in range(2)]
-              + ["mm%d_%d" % (i, n) for i in range(2) for n in range(N)])
+              + ["mm%d_%d" % (i, n) for i in range(2) for n in range(len(WORK) + 1)])
 
 
 def _count(mask):
@@ -48,46 +50,71 @@ def _count(mask):
 def _helpers(T, topo, r):
     core = T.cores[r]
     free = [c for c in range(NCORES) if topo.chip(c) == topo.chip(core) and T.rank_of(c) is None]
-    free.sort(key=lambda c: (topo.die(c) == topo.die(core), c))
-    out = []
-    for offs in RELAY:
-        c = [c for c in free if c not in out and all(topo.may_write(c, T.cores[(r + k) % N]) for k in offs)][0]
-        out.append(c)
+    free.sort(key=lambda c: (topo.die(c) == topo.die(core), sum(topo.may_write(c, d) for d in T.cores), c))
+    used, out = [], []
+    for k in RELAY:
+        two = [c for c in free if c not in used and topo.may_write(c, T.cores[(r + k) % N])][:2]
+        used += two
+        out.append(two)
     return out
 
 
-def _put(g, T, topo, src, dst, buf, a_src, a_dst, sem, mask=None):
+def _view(T, buf, a, w):
+    ap = T[buf][:, a:a + w]
+    return ap.bitcast(dt.uint8) if buf in ("xq", "hq") else ap
+
+
+def _put(g, T, topo, src, dst, buf, a_src, a_dst, w, sem):
     rid, pid, _ = topo.addr(dst)
-    m = topo.mask(src, dst) if mask is None else mask
-    o, i = T[buf][:, a_dst:a_dst + NC], T[buf][:, a_src:a_src + NC]
-    if buf in ("xq", "hq"):
-        o, i = o.bitcast(dt.uint8), i.bitcast(dt.uint8)
-    g.remote_dma(out_ap=o, in_ap=i, remote_sem=sem, local_sem=T.sem.loc, pid=pid, routing_id=rid, dma_engine_mask=m)
+    m = topo.mask(src, dst)
+    g.remote_dma(out_ap=_view(T, buf, a_dst, w), in_ap=_view(T, buf, a_src, w), remote_sem=sem, local_sem=T.sem.loc,
+                 pid=pid, routing_id=rid, dma_engine_mask=m)
     return _count(m)
 
 
-def _chip_mask(T, topo, core, helper):
-    on = topo.mask(core, helper)
+def _feed_masks(T, topo, core, helpers):
+    on = topo.mask(core, helpers[0])
     off = 0
     for c in T.cores:
         if topo.chip(c) != topo.chip(core):
             off |= topo.mask(core, c)
-    return (on & ~off) or on
+    bits = [1 << e for e in range(16) if ((on & ~off) or on) >> e & 1]
+    n = len(bits) // len(helpers)
+    return [sum(bits[i * n:(i + 1) * n]) for i in range(len(helpers))]
+
+
+def _feed(g, T, topo, core, helpers, buf, a, w, sem):
+    masks = _feed_masks(T, topo, core, helpers)
+    trs = []
+    for c, m in zip(helpers, masks):
+        rid, pid, _ = topo.addr(c)
+        trs.append(RemoteDMATransfer(dst_ids=[DstId(rid=rid, pnc=pid)], dma_engine_mask=m, remote_sem=sem,
+                                     src=_view(T, buf, a, w), dst=_view(T, buf, a, w)))
+    g.remote_dma_fused(trs, local_sem=T.sem.loc)
+    return sum(_count(m) for m in masks)
 
 
 def _relay_program(g, core, T, topo):
     for r in range(N):
         hs = _helpers(T, topo, r)
-        if core not in hs:
-            continue
-        a = r * NC
-        n = _count(_chip_mask(T, topo, T.cores[r], core))
-        sent = 0
-        for buf, sem in (("xs", T.sem.rs), ("xq", T.sem.rc)):
-            g.wait_ge(sem, n)
-            for k in RELAY[hs.index(core)]:
-                sent += _put(g, T, topo, core, T.cores[(r + k) % N], buf, a, a, T.sem["ax%d" % r])
-        g.wait_ge(T.sem.loc, sent)
+        for t, k in enumerate(RELAY):
+            for f in range(2):
+                if hs[t][f] != core:
+                    continue
+                n = _count(_feed_masks(T, topo, T.cores[r], [two[f] for two in hs])[t])
+                a = r * NC + f * HC
+                sent = 0
+                for buf in PIECES:
+                    g.wait_ge(T.sem["f%s" % buf], n)
+                    sent += _put(g, T, topo, core, T.cores[(r + k) % N], buf, a, a, HC, T.sem["%sx%d" % ("ab"[f], r)])
+                g.wait_ge(T.sem.loc, sent)
+
+
+def _landing(T, topo, j, rank, f):
+    k = (rank - j) % N
+    if k in RELAY:
+        return len(PIECES) * _count(topo.mask(_helpers(T, topo, j)[RELAY.index(k)][f], T.cores[rank]))
+    return (3 if k == DIRECT[0] else 2) * _count(topo.mask(T.cores[j], T.cores[rank]))
 
 
 def rank_program(g, core, T, topo):
@@ -100,92 +127,109 @@ def rank_program(g, core, T, topo):
     own = rank * NC
     helpers = _helpers(T, topo, rank)
 
-    def bank(i, n, a=0, b=NC):
+    def bank(i, n, a, b):
         c = 512 * (2 * (n % RING) + i)
         return T.ps[:, c + a:c + b]
 
     def part(name, i, a=0, b=NC):
         return T[name][:, i * NC + a:i * NC + b]
 
-    sy.dma_start(T.xb[:], T.x[:]).then_inc(S.ldx, 16)
+    for f in range(2):
+        sy.dma_start(T.xb[:, 4 * HC * f:4 * HC * (f + 1)], T.x[:, 4 * HC * f:4 * HC * (f + 1)]).then_inc(S["ldx%d" % f], 16)
     sy.dma_start(T.w1b[:], T.w1[:]).then_inc(S.ldw1, 16)
     sy.dma_start(T.w2b[:], T.w2[:]).then_inc(S.ldw2, 16)
 
-    v.wait_ge(S.ldx, 16)
-    v.quantize_mx(T.xq[:, own:own + NC], T.xs[:, own:own + NC], T.xb[:]).then_inc(S.qx, 1)
+    for f in range(2):
+        a = own + f * HC
+        v.wait_ge(S["ldx%d" % f], 16)
+        v.quantize_mx(T.xq[:, a:a + HC], T.xs[:, a:a + HC], T.xb[:, 4 * HC * f:4 * HC * (f + 1)]).then_inc(S["qx%d" % f], 1)
     v.wait_ge(S.ldw1, 16)
     v.quantize_mx(T.w1q[:], T.w1s[:], T.w1b[:]).then_inc(S.qw1, 1)
     v.wait_ge(S.ldw2, 16)
     v.quantize_mx(T.w2q[:], T.w2s[:], T.w2b[:]).then_inc(S.qw2, 1)
 
-    g.wait_ge(S.qx, 1)
+    ax = S["ax%d" % rank]
+    first = T.cores[(rank + DIRECT[0]) % N]
     sent = 0
-    for n, k in enumerate(DIRECT):
-        if n == FIRST:
-            for buf, sem in (("xs", S.rs), ("xq", S.rc)):
-                for c in helpers:
-                    sent += _put(g, T, topo, core, c, buf, own, own, sem, _chip_mask(T, topo, core, c))
+    g.wait_ge(S.qx0, 1)
+    sent += _put(g, T, topo, core, first, "xq", own, own, HC, ax)
+    for f in range(2):
+        if f:
+            g.wait_ge(S.qx1, 1)
+        for buf in PIECES:
+            sent += _feed(g, T, topo, core, [two[f] for two in helpers], buf, own + f * HC, HC, S["f%s" % buf])
+    sent += _put(g, T, topo, core, first, "xq", own + HC, own + HC, HC, ax)
+    sent += _put(g, T, topo, core, first, "xs", own, own, NC, ax)
+    for k in DIRECT[1:-1]:
         for buf in ("xq", "xs"):
-            sent += _put(g, T, topo, core, T.cores[(rank + k) % N], buf, own, own, S["ax%d" % rank])
+            sent += _put(g, T, topo, core, T.cores[(rank + k) % N], buf, own, own, NC, ax)
+    for f in range(2):
+        for buf in ("xq", "xs"):
+            sent += _put(g, T, topo, core, T.cores[(rank + DIRECT[-1]) % N], buf, own + f * HC, own + f * HC, HC,
+                         S["%sx%d" % ("ab"[f], rank)])
 
-    te.wait_ge(S.qx, 1)
+    items = [(rank, 0, NC, None, 0)]
+    for k, f in WORK:
+        j = (rank - k) % N
+        if f is None:
+            items.append((j, 0, NC, S["ax%d" % j], _landing(T, topo, j, rank, f)))
+        else:
+            items.append((j, f * HC, (f + 1) * HC, S["%sx%d" % ("ab"[f], j)], _landing(T, topo, j, rank, f)))
+    last = len(items) - 1
+    half0 = max(n for n in range(len(items)) if items[n][1] == 0)
+
+    te.wait_ge(S.qx0, 1)
+    te.wait_ge(S.qx1, 1)
     te.wait_ge(S.qw1, 1)
-    srcs = [rank] + [(rank - k) % N for k in ORDER]
-    for n, j in enumerate(srcs):
+    for n, (j, c0, c1, sem, count) in enumerate(items):
         if n:
-            k = (rank - j) % N
-            sender = T.cores[j]
-            for c, offs in zip(_helpers(T, topo, j), RELAY):
-                if k in offs:
-                    sender = c
-            te.wait_ge(S["ax%d" % j], 2 * _count(topo.mask(sender, core)))
+            te.wait_ge(sem, count)
         for i in range(2):
             if n == RING:
                 te.wait_ge(S["cp%d" % i], 1)
             elif n > RING:
-                te.wait_ge(S["mx%d" % i], n - RING)
-                te.wait_ge(S["mn%d" % i], n - RING)
-            te.matmul_mx(bank(i, n), T.w1q[:, 128 * i:128 * i + 128], T.w1s[:, 128 * i:128 * i + 128],
-                         T.xq[:, j * NC:(j + 1) * NC], T.xs[:, j * NC:(j + 1) * NC], True, True).then_inc(S["mm%d_%d" % (i, n)], 1)
+                for name, _ in FOLDS:
+                    te.wait_ge(S["%s%d" % (name, i)], n - RING)
+            te.matmul_mx(bank(i, n, 0, c1 - c0), T.w1q[:, 128 * i:128 * i + 128], T.w1s[:, 128 * i:128 * i + 128],
+                         T.xq[:, j * NC + c0:j * NC + c1], T.xs[:, j * NC + c0:j * NC + c1], True, True
+                         ).then_inc(S["mm%d_%d" % (i, n)], 1)
 
     for i in range(2):
         sc.wait_ge(S["mm%d_0" % i], 1)
-        sc.activation(part("acc", i), bank(i, 0), ActivationFunctionType.Copy).then_inc(S["cp%d" % i], 1)
+        sc.activation(part("acc", i), bank(i, 0, 0, NC), ActivationFunctionType.Copy).then_inc(S["cp%d" % i], 1)
 
-    for n in range(1, N - 1):
+    def pack(f):
+        v.wait_ge(S["sc%d" % f], 4)
+        v.quantize_mx(T.hq[:, f * HC:(f + 1) * HC], T.hs[:, f * HC:(f + 1) * HC],
+                      T.hb[:, 4 * HC * f:4 * HC * (f + 1)]).then_inc(S["qh%d" % f], 1)
+
+    for n in range(1, last + 1):
+        c0, c1 = items[n][1], items[n][2]
+        if n == half0 + 2:
+            pack(0)
         for i in range(2):
             v.wait_ge(S["mm%d_%d" % (i, n)], 1)
             for name, op in FOLDS:
                 if n == 1:
                     v.wait_ge(S["cp%d" % i], 1)
-                    prev = part("acc", i)
+                    prev = part("acc", i, c0, c1)
                 else:
                     v.wait_ge(S["%s%d" % (name, i)], n - 1)
-                    prev = part(name, i)
-                v.tensor_tensor(part(name, i), bank(i, n), prev, op).then_inc(S["%s%d" % (name, i)], 1)
-    n = N - 1
-    for f in range(2):
-        for i in range(2):
-            v.wait_ge(S["mm%d_%d" % (i, n)], 1)
-            for name, op in FOLDS:
-                v.wait_ge(S["%s%d" % (name, i)], n - 1 + f)
-                m = part(name, i, f * HC, (f + 1) * HC)
-                v.tensor_tensor(m, bank(i, n, f * HC, (f + 1) * HC), m, op).then_inc(S["%s%d" % (name, i)], 1)
+                    prev = part(name, i, c0, c1)
+                v.tensor_tensor(part(name, i, c0, c1), bank(i, n, 0, c1 - c0), prev, op).then_inc(S["%s%d" % (name, i)], 1)
+    pack(1)
 
-    for f in range(2):
+    for f, n in enumerate((half0, last)):
         for b, (name, i) in enumerate(PARTS):
-            sc.wait_ge(S["%s%d" % (name, i)], N - 1 + f)
+            sc.wait_ge(S["%s%d" % (name, i)], n)
             sc.activation(T.hb[:, 4 * HC * f + b:4 * HC * (f + 1):4], part(name, i, f * HC, (f + 1) * HC),
                           ActivationFunctionType.Copy, scale=SCALE).then_inc(S["sc%d" % f], 1)
 
+    before = T.cores[(rank - 1) % N]
     for f in range(2):
-        v.wait_ge(S["sc%d" % f], 4)
-        v.quantize_mx(T.hq[:, f * HC:(f + 1) * HC], T.hs[:, f * HC:(f + 1) * HC],
-                      T.hb[:, 4 * HC * f:4 * HC * (f + 1)]).then_inc(S.qh, 1)
-
-    g.wait_ge(S.qh, 2)
-    for buf in ("hq", "hs"):
-        sent += _put(g, T, topo, core, T.cores[(rank - 1) % N], buf, 0, NC, S.ah)
+        g.wait_ge(S["qh%d" % f], 1)
+        for buf in ("hq", "hs"):
+            sent += _put(g, T, topo, core, before, buf, f * HC, NC + f * HC, HC, S["ah%d" % f])
     g.wait_ge(S.loc, sent)
 
     sc.wait_ge(S.sc0, 4)
@@ -194,12 +238,13 @@ def rank_program(g, core, T, topo):
     sc.dma_start(T.h[:], T.hb[:]).then_inc(S.sth, 16)
 
     te.wait_ge(S.qw2, 1)
-    te.wait_ge(S.qh, 2)
     yp = [T.ps[:, 512 * (YBANK + f):512 * (YBANK + f) + HC] for f in range(2)]
     for t in range(2):
-        if t:
-            te.wait_ge(S.ah, 2 * _count(topo.mask(T.cores[(rank + 1) % N], core)))
         for f in range(2):
+            if t:
+                te.wait_ge(S["ah%d" % f], 2 * _count(topo.mask(T.cores[(rank + 1) % N], core)))
+            else:
+                te.wait_ge(S["qh%d" % f], 1)
             a = t * NC + f * HC
             mm = te.matmul_mx(yp[f], T.w2q[:, 128 * t:128 * t + 128], T.w2s[:, 128 * t:128 * t + 128],
                               T.hq[:, a:a + HC], T.hs[:, a:a + HC], t == 0, t == 1)
@@ -207,10 +252,12 @@ def rank_program(g, core, T, topo):
                 mm.then_inc(S["ym%d" % f], 1)
 
     v.wait_ge(S.ym0, 1)
-    v.tensor_copy(T.yb[:, 0:HC], yp[0]).then_inc(S.yc, 1)
+    v.tensor_copy(T.yb[:, 0:HC], yp[0]).then_inc(S.yc0, 1)
     sc.wait_ge(S.ym1, 1)
-    sc.activation(T.yb[:, HC:NC], yp[1], ActivationFunctionType.Copy).then_inc(S.yc, 1)
-    sy.wait_ge(S.yc, 2)
-    sy.dma_start(T.y[:], T.yb[:]).then_inc(S.sty, 16)
-    sy.wait_ge(S.sty, 16)
+    sc.activation(T.yb[:, HC:NC], yp[1], ActivationFunctionType.Copy).then_inc(S.yc1, 1)
+    for f in range(2):
+        sy.wait_ge(S["yc%d" % f], 1)
+        sy.dma_start(T.y[:, f * HC:(f + 1) * HC], T.yb[:, f * HC:(f + 1) * HC]).then_inc(S["sty%d" % f], 16)
+    for f in range(2):
+        sy.wait_ge(S["sty%d" % f], 16)
     sc.wait_ge(S.sth, 16)

from concourse.bass import DstId, RemoteDMATransfer
from concourse.mybir import dt, AluOpType, ActivationFunctionType

N = 6
NCORES = 128
NC = 256
HC = NC // 2
SCALE = 0.041

DIRECT = (1, 2, 5)
RELAY = (3, 4)
WORK = ((1, None), (2, None), (5, 0), (3, 0), (4, 0), (3, 1), (4, 1), (5, 1))
RING = 3
YBANK = 2 * RING
FOLDS = (("mx", AluOpType.max), ("mn", AluOpType.min))
PARTS = (("mx", 0), ("mn", 0), ("mx", 1), ("mn", 1))
PIECES = ("xs", "xq")

SCRATCH = {
    "xb": ("sbuf", [128, 4 * NC], "bfloat16"),
    "w1b": ("sbuf", [128, 1024], "bfloat16"),
    "w2b": ("sbuf", [128, 1024], "bfloat16"),
    "xq": ("sbuf", [128, N * NC], "float8_e4m3fn_x4"),
    "xs": ("sbuf", [128, N * NC], "uint8"),
    "w1q": ("sbuf", [128, 256], "float8_e4m3fn_x4"),
    "w1s": ("sbuf", [128, 256], "uint8"),
    "w2q": ("sbuf", [128, 256], "float8_e4m3fn_x4"),
    "w2s": ("sbuf", [128, 256], "uint8"),
    "acc": ("sbuf", [128, 2 * NC], "float32"),
    "mx": ("sbuf", [128, 2 * NC], "float32"),
    "mn": ("sbuf", [128, 2 * NC], "float32"),
    "hb": ("sbuf", [128, 4 * NC], "bfloat16"),
    "hq": ("sbuf", [128, 2 * NC], "float8_e4m3fn_x4"),
    "hs": ("sbuf", [128, 2 * NC], "uint8"),
    "yb": ("sbuf", [128, NC], "float32"),
    "ps": ("psum", [128, 512 * (YBANK + 2)], "float32"),
}
SEMAPHORES = (["ldx0", "ldx1", "ldw1", "ldw2", "qx0", "qx1", "qw1", "qw2", "qh0", "qh1", "loc", "ah0", "ah1", "sc0", "sc1",
               "ym0", "ym1", "yc0", "yc1", "sty0", "sty1", "sth"]
              + ["f%s" % p for p in PIECES]
              + ["%sx%d" % (s, j) for s in "ab" for j in range(N)]
              + ["%s%d" % (s, i) for s in ("cp", "mx", "mn") for i in range(2)]
              + ["mm%d_%d" % (i, n) for i in range(2) for n in range(len(WORK) + 1)])


def _count(mask):
    return bin(mask).count("1")


def _helpers(T, topo, r):
    core = T.cores[r]
    free = [c for c in range(NCORES) if topo.chip(c) == topo.chip(core) and T.rank_of(c) is None]
    free.sort(key=lambda c: (topo.die(c) == topo.die(core), sum(topo.may_write(c, d) for d in T.cores), c))
    used, out = [], []
    for k in RELAY:
        two = [c for c in free if c not in used and topo.may_write(c, T.cores[(r + k) % N])][:2]
        used += two
        out.append(two)
    return out


def _view(T, buf, a, w):
    ap = T[buf][:, a:a + w]
    return ap.bitcast(dt.uint8) if buf in ("xq", "hq") else ap


def _put(g, T, topo, src, dst, buf, a_src, a_dst, w, sem):
    rid, pid, _ = topo.addr(dst)
    m = topo.mask(src, dst)
    g.remote_dma(out_ap=_view(T, buf, a_dst, w), in_ap=_view(T, buf, a_src, w), remote_sem=sem, local_sem=T.sem.loc,
                 pid=pid, routing_id=rid, dma_engine_mask=m)
    return _count(m)


def _feed_masks(T, topo, core, helpers):
    on = topo.mask(core, helpers[0])
    off = 0
    for c in T.cores:
        if topo.chip(c) != topo.chip(core):
            off |= topo.mask(core, c)
    bits = [1 << e for e in range(16) if ((on & ~off) or on) >> e & 1]
    n = len(bits) // len(helpers)
    return [sum(bits[i * n:(i + 1) * n]) for i in range(len(helpers))]


def _feed(g, T, topo, core, helpers, buf, a, w, sem):
    masks = _feed_masks(T, topo, core, helpers)
    trs = []
    for c, m in zip(helpers, masks):
        rid, pid, _ = topo.addr(c)
        trs.append(RemoteDMATransfer(dst_ids=[DstId(rid=rid, pnc=pid)], dma_engine_mask=m, remote_sem=sem,
                                     src=_view(T, buf, a, w), dst=_view(T, buf, a, w)))
    g.remote_dma_fused(trs, local_sem=T.sem.loc)
    return sum(_count(m) for m in masks)


def _relay_program(g, core, T, topo):
    for r in range(N):
        hs = _helpers(T, topo, r)
        for t, k in enumerate(RELAY):
            for f in range(2):
                if hs[t][f] != core:
                    continue
                n = _count(_feed_masks(T, topo, T.cores[r], [two[f] for two in hs])[t])
                a = r * NC + f * HC
                sent = 0
                for buf in PIECES:
                    g.wait_ge(T.sem["f%s" % buf], n)
                    sent += _put(g, T, topo, core, T.cores[(r + k) % N], buf, a, a, HC, T.sem["%sx%d" % ("ab"[f], r)])
                g.wait_ge(T.sem.loc, sent)


def _landing(T, topo, j, rank, f):
    k = (rank - j) % N
    if k in RELAY:
        return len(PIECES) * _count(topo.mask(_helpers(T, topo, j)[RELAY.index(k)][f], T.cores[rank]))
    return (3 if k == DIRECT[0] else 2) * _count(topo.mask(T.cores[j], T.cores[rank]))


def rank_program(g, core, T, topo):
    rank = T.rank_of(core)
    if rank is None:
        _relay_program(g, core, T, topo)
        return
    S = T.sem
    v, te, sc, sy = g.vector, g.tensor, g.scalar, g.sync
    own = rank * NC
    helpers = _helpers(T, topo, rank)

    def bank(i, n, a, b):
        c = 512 * (2 * (n % RING) + i)
        return T.ps[:, c + a:c + b]

    def part(name, i, a=0, b=NC):
        return T[name][:, i * NC + a:i * NC + b]

    for f in range(2):
        sy.dma_start(T.xb[:, 4 * HC * f:4 * HC * (f + 1)], T.x[:, 4 * HC * f:4 * HC * (f + 1)]).then_inc(S["ldx%d" % f], 16)
    sy.dma_start(T.w1b[:], T.w1[:]).then_inc(S.ldw1, 16)
    sy.dma_start(T.w2b[:], T.w2[:]).then_inc(S.ldw2, 16)

    for f in range(2):
        a = own + f * HC
        v.wait_ge(S["ldx%d" % f], 16)
        v.quantize_mx(T.xq[:, a:a + HC], T.xs[:, a:a + HC], T.xb[:, 4 * HC * f:4 * HC * (f + 1)]).then_inc(S["qx%d" % f], 1)
    v.wait_ge(S.ldw1, 16)
    v.quantize_mx(T.w1q[:], T.w1s[:], T.w1b[:]).then_inc(S.qw1, 1)
    v.wait_ge(S.ldw2, 16)
    v.quantize_mx(T.w2q[:], T.w2s[:], T.w2b[:]).then_inc(S.qw2, 1)

    ax = S["ax%d" % rank]
    first = T.cores[(rank + DIRECT[0]) % N]
    sent = 0
    g.wait_ge(S.qx0, 1)
    sent += _put(g, T, topo, core, first, "xq", own, own, HC, ax)
    for f in range(2):
        if f:
            g.wait_ge(S.qx1, 1)
        for buf in PIECES:
            sent += _feed(g, T, topo, core, [two[f] for two in helpers], buf, own + f * HC, HC, S["f%s" % buf])
    sent += _put(g, T, topo, core, first, "xq", own + HC, own + HC, HC, ax)
    sent += _put(g, T, topo, core, first, "xs", own, own, NC, ax)
    for k in DIRECT[1:-1]:
        for buf in ("xq", "xs"):
            sent += _put(g, T, topo, core, T.cores[(rank + k) % N], buf, own, own, NC, ax)
    for f in range(2):
        for buf in ("xq", "xs"):
            sent += _put(g, T, topo, core, T.cores[(rank + DIRECT[-1]) % N], buf, own + f * HC, own + f * HC, HC,
                         S["%sx%d" % ("ab"[f], rank)])

    items = [(rank, 0, NC, None, 0)]
    for k, f in WORK:
        j = (rank - k) % N
        if f is None:
            items.append((j, 0, NC, S["ax%d" % j], _landing(T, topo, j, rank, f)))
        else:
            items.append((j, f * HC, (f + 1) * HC, S["%sx%d" % ("ab"[f], j)], _landing(T, topo, j, rank, f)))
    last = len(items) - 1
    half0 = max(n for n in range(len(items)) if items[n][1] == 0)

    te.wait_ge(S.qx0, 1)
    te.wait_ge(S.qx1, 1)
    te.wait_ge(S.qw1, 1)
    for n, (j, c0, c1, sem, count) in enumerate(items):
        if n:
            te.wait_ge(sem, count)
        for i in range(2):
            if n == RING:
                te.wait_ge(S["cp%d" % i], 1)
            elif n > RING:
                for name, _ in FOLDS:
                    te.wait_ge(S["%s%d" % (name, i)], n - RING)
            te.matmul_mx(bank(i, n, 0, c1 - c0), T.w1q[:, 128 * i:128 * i + 128], T.w1s[:, 128 * i:128 * i + 128],
                         T.xq[:, j * NC + c0:j * NC + c1], T.xs[:, j * NC + c0:j * NC + c1], True, True
                         ).then_inc(S["mm%d_%d" % (i, n)], 1)

    for i in range(2):
        sc.wait_ge(S["mm%d_0" % i], 1)
        sc.activation(part("acc", i), bank(i, 0, 0, NC), ActivationFunctionType.Copy).then_inc(S["cp%d" % i], 1)

    def pack(f):
        v.wait_ge(S["sc%d" % f], 4)
        v.quantize_mx(T.hq[:, f * HC:(f + 1) * HC], T.hs[:, f * HC:(f + 1) * HC],
                      T.hb[:, 4 * HC * f:4 * HC * (f + 1)]).then_inc(S["qh%d" % f], 1)

    for n in range(1, last + 1):
        c0, c1 = items[n][1], items[n][2]
        if n == half0 + 2:
            pack(0)
        for i in range(2):
            v.wait_ge(S["mm%d_%d" % (i, n)], 1)
            for name, op in FOLDS:
                if n == 1:
                    v.wait_ge(S["cp%d" % i], 1)
                    prev = part("acc", i, c0, c1)
                else:
                    v.wait_ge(S["%s%d" % (name, i)], n - 1)
                    prev = part(name, i, c0, c1)
                v.tensor_tensor(part(name, i, c0, c1), bank(i, n, 0, c1 - c0), prev, op).then_inc(S["%s%d" % (name, i)], 1)
    pack(1)

    for f, n in enumerate((half0, last)):
        for b, (name, i) in enumerate(PARTS):
            sc.wait_ge(S["%s%d" % (name, i)], n)
            sc.activation(T.hb[:, 4 * HC * f + b:4 * HC * (f + 1):4], part(name, i, f * HC, (f + 1) * HC),
                          ActivationFunctionType.Copy, scale=SCALE).then_inc(S["sc%d" % f], 1)

    before = T.cores[(rank - 1) % N]
    for f in range(2):
        g.wait_ge(S["qh%d" % f], 1)
        for buf in ("hq", "hs"):
            sent += _put(g, T, topo, core, before, buf, f * HC, NC + f * HC, HC, S["ah%d" % f])
    g.wait_ge(S.loc, sent)

    sc.wait_ge(S.sc0, 4)
    sc.wait_ge(S.sc1, 4)
    sc.wait_ge(S.loc, sent)
    sc.dma_start(T.h[:], T.hb[:]).then_inc(S.sth, 16)

    te.wait_ge(S.qw2, 1)
    yp = [T.ps[:, 512 * (YBANK + f):512 * (YBANK + f) + HC] for f in range(2)]
    for t in range(2):
        for f in range(2):
            if t:
                te.wait_ge(S["ah%d" % f], 2 * _count(topo.mask(T.cores[(rank + 1) % N], core)))
            else:
                te.wait_ge(S["qh%d" % f], 1)
            a = t * NC + f * HC
            mm = te.matmul_mx(yp[f], T.w2q[:, 128 * t:128 * t + 128], T.w2s[:, 128 * t:128 * t + 128],
                              T.hq[:, a:a + HC], T.hs[:, a:a + HC], t == 0, t == 1)
            if t:
                mm.then_inc(S["ym%d" % f], 1)

    v.wait_ge(S.ym0, 1)
    v.tensor_copy(T.yb[:, 0:HC], yp[0]).then_inc(S.yc0, 1)
    sc.wait_ge(S.ym1, 1)
    sc.activation(T.yb[:, HC:NC], yp[1], ActivationFunctionType.Copy).then_inc(S.yc1, 1)
    for f in range(2):
        sy.wait_ge(S["yc%d" % f], 1)
        sy.dma_start(T.y[:, f * HC:(f + 1) * HC], T.yb[:, f * HC:(f + 1) * HC]).then_inc(S["sty%d" % f], 16)
    for f in range(2):
        sy.wait_ge(S["sty%d" % f], 16)
    sc.wait_ge(S.sth, 16)
